import numpy as np
import ml_dtypes


def mxq(x, axis, fmt="e4m3"):
    dtype, down = {"e4m3": (ml_dtypes.float8_e4m3fn, 7), "e5m2": (ml_dtypes.float8_e5m2, 14)}[fmt]
    v = np.moveaxis(np.asarray(x, np.float32).astype(ml_dtypes.bfloat16).astype(np.float64), axis, -1)
    blocks = v.reshape(v.shape[:-1] + (-1, 32))
    amax = np.abs(blocks).max(-1, keepdims=True)
    byte = np.maximum(np.where(amax > 0, np.frexp(amax)[1] - 1 + 127, 0) - down, 1)
    scale = np.exp2(byte - 127.0)
    codes = (blocks / scale).astype(np.float32).astype(dtype).astype(np.float64)
    return np.moveaxis((codes * scale).reshape(v.shape), -1, axis)


WIDE = False


def mx_kscale(k):
    if not WIDE:
        return np.ones(k)
    levels = np.array([10, -10, 5, -5, 0])
    if k % 512:
        return np.exp2(np.random.permutation(np.resize(levels, k // 32))).repeat(32)
    a = np.empty((k // 512, 16))
    for p in range(k // 512):
        a[p, :8] = np.random.permutation(np.resize(levels, 8))
        for g in range(8):
            far = levels[np.abs(levels - a[p, g]) >= 10]
            a[p, g + 8] = far[np.random.randint(len(far))]
    return np.exp2(a.ravel()).repeat(32)


def f64(x):
    return np.asarray(x).astype(np.float64)


def striped(idx):
    return np.tile(idx.reshape(-1, 16).T, (8, 1)).astype(np.uint16)


def unstriped(offs):
    return offs[:16].T.reshape(-1).astype(np.int64)


def pack_weight(w):
    k, n = w.shape
    w = f64(np.asarray(w, np.float32).astype(ml_dtypes.bfloat16)).reshape(k // 32, 32, n)
    amax = np.abs(w).max(1)
    byte = np.clip(np.where(amax > 0, np.frexp(amax)[1] - 1 + 127 - 7, 1), 1, 254)
    scaled = (w * np.exp2(127.0 - byte)[:, None, :]).reshape(k, n).astype(np.float32)
    words = np.ascontiguousarray(scaled.reshape(k // 512, 128, 4, n).transpose(0, 1, 3, 2)).astype(ml_dtypes.float8_e4m3fn).view(np.uint8)
    return words, np.ascontiguousarray(byte.astype(np.uint8).reshape(k // 512, 16, n))


def unpack_weight(words, scales):
    g, p, n, _ = words.shape
    vals = np.ascontiguousarray(words).view(ml_dtypes.float8_e4m3fn).astype(np.float64) * np.repeat(np.exp2(scales.astype(np.float64) - 127.0), 8, axis=1)[..., None]
    return vals.transpose(0, 1, 3, 2).reshape(g * 512, n)


K, T, S, V, D = 512, 2048, 512, 512, 4


def setup_inputs():
    n = np.random.standard_normal
    s = mx_kscale(K)[:, None]
    packed_xT = pack_weight(n((K, T)) * s)
    packed_eT = pack_weight(n((K, T)) * s)
    return {
        "x_words": packed_xT[0],
        "x_scales": packed_xT[1],
        "e_words": packed_eT[0],
        "e_scales": packed_eT[1],
        "hT": (n((K, V)) / np.sqrt(K) / s).astype(np.float32),
        "gT": (n((K, V)) / np.sqrt(K) / s).astype(np.float32),
        "lr": (np.random.uniform(0.3, 1.0, (V, 1))).astype(np.float32),
        "offs": striped(np.random.permutation(T)[:S]),
    }


def reference(x_words, x_scales, e_words, e_scales, hT, gT, lr, offs):
    hTq = mxq(f64(hT), 0, "e4m3")
    xq = unpack_weight(x_words, x_scales)[:, unstriped(offs)]
    y = hTq.T @ xq
    gTq = mxq(f64(gT), 0, "e4m3")
    e_offs = unpack_weight(e_words, e_scales)[:, unstriped(offs)]
    z = gTq.T @ e_offs
    p = f64(lr) * (y * z)
    ss = p.reshape(len(p), -1, D).sum(axis=2)
    p2 = (p) ** 2
    return ss / (np.sqrt(p2.reshape(len(p2), -1, D).sum(axis=2) + 0.1))

@@ -1,0 +1,159 @@
+from contextlib import ExitStack
+
+import concourse.mybir as mybir
+from concourse.masks import make_identity
+
+K, T, S, V, D = 512, 2048, 512, 512, 4
+FLOPS = 2 * 2 * K * V * S
+
+F32 = mybir.dt.float32
+BF16 = mybir.dt.bfloat16
+I32 = mybir.dt.int32
+U32 = mybir.dt.uint32
+U16 = mybir.dt.uint16
+U8 = mybir.dt.uint8
+FP8X4 = mybir.dt.float8_e4m3fn_x4
+ACT = mybir.ActivationFunctionType
+MULT = mybir.AluOpType.mult
+
+P = 128
+PACK = 4
+NB = V // P
+G = S // D
+
+
+def tile_picked_yghost_norm_p_kernel(tc, x_words, x_scales, e_words, e_scales, hT, gT, lr, offs, out):
+    nc = tc.nc
+    with ExitStack() as ctx:
+        keep = ctx.enter_context(tc.tile_pool(name="keep", bufs=1))
+        psum = ctx.enter_context(tc.psum_pool(name="psum", bufs=1))
+
+        offsets = keep.tile([P, S // 16], U16, name="offsets")
+        nc.sync.dma_start(offsets[:], offs)
+
+        def scale_table(name, eng):
+            t = keep.tile([P, T], U8, name=name, align_bytes=64)
+            eng.memset(t[:].bitcast(I32), 0)
+            return t
+
+        def load_scales(t, src, queue):
+            for q in range(4):
+                queue.dma_start(out=t[32 * q : 32 * q + 4, :].bitcast(I32), in_=src[0, 4 * q : 4 * q + 4, :].bitcast(I32))
+
+        def load_words(name, src):
+            t = keep.tile([P, T], I32, name=name, align_bytes=64)
+            nc.sync.dma_start(out=t[:], in_=src[0].rearrange("p n t -> p (n t)").bitcast(I32))
+            return t
+
+        def load_block(name, src, b):
+            t = keep.tile([P, PACK, P], F32, name=name)
+            nc.sync.dma_start(out=t[:], in_=src[:, b * P : (b + 1) * P].rearrange("(p j) w -> p j w", j=PACK))
+            return t
+
+        def gather_scales(name, table):
+            picked = keep.tile([P, S], U8, name=name + "_picked", align_bytes=64)
+            nc.vector.tensor_copy(out=picked[:], in_=table[:].indirect(offsets[:]))
+            planes = keep.tile([P, D, G], U8, name=name + "_planes", align_bytes=64)
+            nc.vector.tensor_copy(out=planes[:].rearrange("p d v -> p v d"), in_=picked[:].rearrange("p (v d) -> p v d", d=D))
+            return planes
+
+        def gather_words(name, table):
+            planes = keep.tile([P, D, G], U32, name=name, align_bytes=64)
+            nc.vector.tensor_copy(out=planes[:].rearrange("p d v -> p v d"), in_=table[:].bitcast(U32).indirect(offsets[:]))
+            return planes
+
+        def cast(name, raw, on_scalar):
+            grouped = keep.tile([P, P, PACK], BF16, name=name, align_bytes=64)
+            if on_scalar:
+                nc.scalar.copy(out=grouped[:], in_=raw[:].rearrange("p j w -> p w j"))
+            else:
+                nc.vector.tensor_copy(out=grouped[:], in_=raw[:].rearrange("p j w -> p w j"))
+            return grouped
+
+        def quantise(name, grouped):
+            codes = keep.tile([P, P], U32, name=name + "_codes", align_bytes=64)
+            scales = keep.tile([P, P], U8, name=name + "_scales", align_bytes=64)
+            nc.vector.quantize_mx(out=codes[:].bitcast(FP8X4), scales=scales[:], in_=grouped[:].rearrange("p w j -> p (w j)"))
+            return codes, scales
+
+        def product(tag, bufs, words, bytes_, q):
+            acc = psum.tile([P, D, P], F32, name=tag, tag=tag, bufs=bufs)
+            for d in range(D):
+                nc.tensor.matmul_mx(out=acc[:, d, :], lhsT=words[:, d, :].bitcast(FP8X4), lhsT_scale=bytes_[:, d, :],
+                                    rhs=q[0][:].bitcast(FP8X4), rhs_scale=q[1][:], start=True, stop=True)
+            return acc
+
+        xs = scale_table("xs", nc.vector)
+        es = scale_table("es", nc.gpsimd)
+        step = keep.tile([P, NB], F32, name="step")
+        with nc.allow_non_contiguous_dma(reason="one step size a partition"):
+            nc.gpsimd.dma_start(out=step[:], in_=lr.rearrange("(b p) o -> p (b o)", p=P))
+        h_raw = [None] * NB
+        g_raw = [None] * NB
+        h_raw[0] = load_block("h0", hT, 0)
+        h_raw[1] = load_block("h1", hT, 1)
+        h_raw[2] = load_block("h2", hT, 2)
+        load_scales(xs, x_scales, nc.sync)
+        xw = load_words("xw", x_words)
+        load_scales(es, e_scales, nc.sync)
+        g_raw[0] = load_block("g0", gT, 0)
+        ew = load_words("ew", e_words)
+        g_raw[1] = load_block("g1", gT, 1)
+        h_raw[3] = load_block("h3", hT, 3)
+        g_raw[2] = load_block("g2", gT, 2)
+        g_raw[3] = load_block("g3", gT, 3)
+
+        warm = keep.tile([P, 2], F32, name="warm")
+        nc.gpsimd.memset(warm[:, 0:1], 1.0)
+        nc.scalar.activation(out=warm[:, 1:2], in_=warm[:, 0:1], func=ACT.Abs_reciprocal_sqrt)
+
+        ident = keep.tile([P, P], F32, name="ident")
+        make_identity(nc, ident[:])
+        step2 = keep.tile([P, NB], F32, name="step2")
+        nc.gpsimd.tensor_tensor(out=step2[:], in0=step[:], in1=step[:], op=MULT)
+
+        x_bytes = gather_scales("xb", xs)
+        x_planes = gather_words("xp", xw)
+
+        y_sb = [None] * NB
+
+        def y_block(b, on_scalar):
+            hq = quantise("hq%d" % b, cast("hc%d" % b, h_raw[b], on_scalar))
+            acc = product("y", 2, x_planes, x_bytes, hq)
+            y_sb[b] = keep.tile([P, D, P], F32, name="y%d" % b)
+            nc.scalar.copy(out=y_sb[b][:], in_=acc[:])
+
+        def z_block(b, on_scalar):
+            gq = quantise("gq%d" % b, cast("gc%d" % b, g_raw[b], on_scalar))
+            acc = product("z", 3, e_planes, e_bytes, gq)
+            terms = keep.tile([P, D, P], F32, name="terms%d" % b)
+            nc.vector.tensor_tensor(out=terms[:], in0=acc[:], in1=y_sb[b][:], op=MULT)
+            squares = keep.tile([P, D, P], F32, name="squares%d" % b)
+            nc.scalar.activation(out=squares[:], in_=terms[:], func=ACT.Square)
+            return terms, squares
+
+        def finish(b, terms, squares):
+            sums = psum.tile([P, 2, G], F32, name="sums", tag="sums", bufs=3)
+            for i, src in enumerate((terms, squares)):
+                for d in range(D):
+                    nc.tensor.matmul(out=sums[:, i, :], lhsT=src[:, d, :], rhs=ident[:], is_transpose=True, start=(d == 0), stop=(d == D - 1))
+            inv = keep.tile([P, G], F32, name="inv%d" % b)
+            nc.scalar.activation(out=inv[:], in_=sums[:, 1, :], func=ACT.Abs_reciprocal_sqrt, scale=step2[:, b : b + 1], bias=0.1)
+            res = keep.tile([P, G], F32, name="res%d" % b)
+            nc.vector.scalar_tensor_tensor(out=res[:], in0=sums[:, 0, :], scalar=step[:, b : b + 1], in1=inv[:], op0=MULT, op1=MULT)
+            nc.sync.dma_start(out=out[b * P : (b + 1) * P, :], in_=res[:])
+
+        y_block(0, True)
+        y_block(1, True)
+        y_block(2, True)
+        e_bytes = gather_scales("eb", es)
+        e_planes = gather_words("ep", ew)
+        t0 = z_block(0, True)
+        t1 = z_block(1, True)
+        y_block(3, False)
+        finish(0, *t0)
+        t2 = z_block(2, True)
+        finish(1, *t1)
+        t3 = z_block(3, True)
+        finish(2, *t2)
+        finish(3, *t3)

@@ -1,7 +1,6 @@
 from contextlib import ExitStack
 
 import concourse.mybir as mybir
-from concourse.masks import make_identity
 
 K, T, S, V, D = 512, 2048, 512, 512, 4
 FLOPS = 2 * 2 * K * V * S
@@ -15,6 +14,7 @@ U8 = mybir.dt.uint8
 FP8X4 = mybir.dt.float8_e4m3fn_x4
 ACT = mybir.ActivationFunctionType
 MULT = mybir.AluOpType.mult
+ADD = mybir.AluOpType.add
 
 P = 128
 PACK = 4
@@ -46,28 +46,33 @@ def tile_picked_yghost_norm_p_kernel(tc, x_words, x_scales, e_words, e_scales, h
             return t
 
         def load_block(name, src, b):
-            t = keep.tile([P, PACK, P], F32, name=name)
+            t = keep.tile([P, PACK, P], F32, name=name, tag=name, align_bytes=64)
             nc.sync.dma_start(out=t[:], in_=src[:, b * P : (b + 1) * P].rearrange("(p j) w -> p j w", j=PACK))
             return t
 
+        def load_steps(queue):
+            with nc.allow_non_contiguous_dma(reason="one step size a partition"):
+                queue.dma_start(out=step[:], in_=lr.rearrange("(b p) o -> p (b o)", p=P))
+
         def gather_scales(name, table):
-            picked = keep.tile([P, S], U8, name=name + "_picked", align_bytes=64)
+            picked = keep.tile([P, S], U8, name=name, align_bytes=64)
             nc.vector.tensor_copy(out=picked[:], in_=table[:].indirect(offsets[:]))
-            planes = keep.tile([P, D, G], U8, name=name + "_planes", align_bytes=64)
-            nc.vector.tensor_copy(out=planes[:].rearrange("p d v -> p v d"), in_=picked[:].rearrange("p (v d) -> p v d", d=D))
-            return planes
+            return picked
 
         def gather_words(name, table):
-            planes = keep.tile([P, D, G], U32, name=name, align_bytes=64)
-            nc.vector.tensor_copy(out=planes[:].rearrange("p d v -> p v d"), in_=table[:].bitcast(U32).indirect(offsets[:]))
-            return planes
+            picked = keep.tile([P, S], U32, name=name, align_bytes=64)
+            nc.vector.tensor_copy(out=picked[:], in_=table[:].bitcast(U32).indirect(offsets[:]))
+            return picked
 
-        def cast(name, raw, on_scalar):
-            grouped = keep.tile([P, P, PACK], BF16, name=name, align_bytes=64)
-            if on_scalar:
-                nc.scalar.copy(out=grouped[:], in_=raw[:].rearrange("p j w -> p w j"))
+        def cast(name, raw, eng):
+            grouped = keep.tile([P, P, PACK], BF16, name=name, tag=name, align_bytes=64)
+            dst, src = grouped[:], raw[:].rearrange("p j w -> p w j")
+            if eng == "S":
+                nc.scalar.copy(out=dst, in_=src)
+            elif eng == "G":
+                nc.gpsimd.tensor_copy(out=dst, in_=src)
             else:
-                nc.vector.tensor_copy(out=grouped[:], in_=raw[:].rearrange("p j w -> p w j"))
+                nc.vector.tensor_copy(out=dst, in_=src)
             return grouped
 
         def quantise(name, grouped):
@@ -77,83 +82,93 @@ def tile_picked_yghost_norm_p_kernel(tc, x_words, x_scales, e_words, e_scales, h
             return codes, scales
 
         def product(tag, bufs, words, bytes_, q):
-            acc = psum.tile([P, D, P], F32, name=tag, tag=tag, bufs=bufs)
-            for d in range(D):
-                nc.tensor.matmul_mx(out=acc[:, d, :], lhsT=words[:, d, :].bitcast(FP8X4), lhsT_scale=bytes_[:, d, :],
-                                    rhs=q[0][:].bitcast(FP8X4), rhs_scale=q[1][:], start=True, stop=True)
-            return acc
+            acc = psum.tile([P, S], F32, name=tag, tag=tag, bufs=bufs)
+            nc.tensor.matmul_mx(out=acc[:], lhsT=q[0][:].bitcast(FP8X4), lhsT_scale=q[1][:],
+                                rhs=words[:].bitcast(FP8X4), rhs_scale=bytes_[:], start=True, stop=True)
+            return acc[:].rearrange("p (v d) -> p d v", d=D)
 
         xs = scale_table("xs", nc.vector)
         es = scale_table("es", nc.gpsimd)
         step = keep.tile([P, NB], F32, name="step")
-        with nc.allow_non_contiguous_dma(reason="one step size a partition"):
-            nc.gpsimd.dma_start(out=step[:], in_=lr.rearrange("(b p) o -> p (b o)", p=P))
+
         h_raw = [None] * NB
         g_raw = [None] * NB
         h_raw[0] = load_block("h0", hT, 0)
-        h_raw[1] = load_block("h1", hT, 1)
-        h_raw[2] = load_block("h2", hT, 2)
+        g_raw[0] = load_block("g0", gT, 0)
         load_scales(xs, x_scales, nc.sync)
         xw = load_words("xw", x_words)
         load_scales(es, e_scales, nc.sync)
-        g_raw[0] = load_block("g0", gT, 0)
         ew = load_words("ew", e_words)
+        load_steps(nc.sync)
+        h_raw[1] = load_block("h1", hT, 1)
         g_raw[1] = load_block("g1", gT, 1)
-        h_raw[3] = load_block("h3", hT, 3)
+        h_raw[2] = load_block("h2", hT, 2)
         g_raw[2] = load_block("g2", gT, 2)
+        h_raw[3] = load_block("h3", hT, 3)
         g_raw[3] = load_block("g3", gT, 3)
 
         warm = keep.tile([P, 2], F32, name="warm")
         nc.gpsimd.memset(warm[:, 0:1], 1.0)
         nc.scalar.activation(out=warm[:, 1:2], in_=warm[:, 0:1], func=ACT.Abs_reciprocal_sqrt)
 
-        ident = keep.tile([P, P], F32, name="ident")
-        make_identity(nc, ident[:])
-        step2 = keep.tile([P, NB], F32, name="step2")
-        nc.gpsimd.tensor_tensor(out=step2[:], in0=step[:], in1=step[:], op=MULT)
 
-        x_bytes = gather_scales("xb", xs)
-        x_planes = gather_words("xp", xw)
+        CAST = "SSSSSVVV"
+        ROUTE = "VVVV"
+        SLOT = {"y1":"h2","y2":"h3","squares0":"hc3","terms0":"gc1","terms1":"gc2","halves0":"gc3"}
 
-        y_sb = [None] * NB
+        def tile(name, shape):
+            return keep.tile(shape, F32, name=name, tag=SLOT.get(name, name), align_bytes=64)
 
-        def y_block(b, on_scalar):
-            hq = quantise("hq%d" % b, cast("hc%d" % b, h_raw[b], on_scalar))
-            acc = product("y", 2, x_planes, x_bytes, hq)
-            y_sb[b] = keep.tile([P, D, P], F32, name="y%d" % b)
-            nc.scalar.copy(out=y_sb[b][:], in_=acc[:])
+        hq = [None] * NB
+        gq = [None] * NB
+        y_ps = [None] * NB
+        z_ps = [None] * NB
+        terms = [None] * NB
+        squares = [None] * NB
 
-        def z_block(b, on_scalar):
-            gq = quantise("gq%d" % b, cast("gc%d" % b, g_raw[b], on_scalar))
-            acc = product("z", 3, e_planes, e_bytes, gq)
-            terms = keep.tile([P, D, P], F32, name="terms%d" % b)
-            nc.vector.tensor_tensor(out=terms[:], in0=acc[:], in1=y_sb[b][:], op=MULT)
-            squares = keep.tile([P, D, P], F32, name="squares%d" % b)
-            nc.scalar.activation(out=squares[:], in_=terms[:], func=ACT.Square)
-            return terms, squares
+        def prepare(b):
+            hc = cast("hc%d" % b, h_raw[b], CAST[b])
+            gc = cast("gc%d" % b, g_raw[b], CAST[NB + b])
+            hq[b] = quantise("hq%d" % b, hc)
+            gq[b] = quantise("gq%d" % b, gc)
 
-        def finish(b, terms, squares):
-            sums = psum.tile([P, 2, G], F32, name="sums", tag="sums", bufs=3)
-            for i, src in enumerate((terms, squares)):
-                for d in range(D):
-                    nc.tensor.matmul(out=sums[:, i, :], lhsT=src[:, d, :], rhs=ident[:], is_transpose=True, start=(d == 0), stop=(d == D - 1))
-            inv = keep.tile([P, G], F32, name="inv%d" % b)
-            nc.scalar.activation(out=inv[:], in_=sums[:, 1, :], func=ACT.Abs_reciprocal_sqrt, scale=step2[:, b : b + 1], bias=0.1)
-            res = keep.tile([P, G], F32, name="res%d" % b)
-            nc.vector.scalar_tensor_tensor(out=res[:], in0=sums[:, 0, :], scalar=step[:, b : b + 1], in1=inv[:], op0=MULT, op1=MULT)
+        def multiply(b):
+            y_ps[b] = product("y", 4, x_picked, x_bytes, hq[b])
+            z_ps[b] = product("z", 4, e_picked, e_bytes, gq[b])
+
+        def combine(b):
+            y_sb = tile("y%d" % b, [P, D, G])
+            nc.scalar.copy(out=y_sb[:], in_=y_ps[b])
+            terms[b] = tile("terms%d" % b, [P, D, G])
+            nc.vector.scalar_tensor_tensor(out=terms[b][:], in0=z_ps[b], scalar=step[:, b : b + 1], in1=y_sb[:], op0=MULT, op1=MULT)
+            squares[b] = tile("squares%d" % b, [P, D, G])
+            nc.scalar.activation(out=squares[b][:], in_=terms[b][:], func=ACT.Square)
+
+        def finish(b):
+            finish_on_vector(b)
+
+        def finish_on_vector(b):
+            halves = tile("halves%d" % b, [P, 2, 2, G])
+            for i, src in enumerate((terms[b], squares[b])):
+                nc.vector.tensor_tensor(out=halves[:, i], in0=src[:, 0:2, :], in1=src[:, 2:4, :], op=ADD) if i == 0 else nc.vector.tensor_tensor(out=halves[:, i], in0=src[:, 0:2, :], in1=src[:, 2:4, :], op=ADD)
+            sums = tile("sums%d" % b, [P, 2, G])
+            nc.vector.tensor_tensor(out=sums[:], in0=halves[:, :, 0, :], in1=halves[:, :, 1, :], op=ADD)
+            inv = tile("inv%d" % b, [P, G])
+            nc.scalar.activation(out=inv[:], in_=sums[:, 1, :], func=ACT.Abs_reciprocal_sqrt, bias=0.1)
+            res = tile("res%d" % b, [P, G])
+            nc.vector.tensor_tensor(out=res[:], in0=sums[:, 0, :], in1=inv[:], op=MULT)
             nc.sync.dma_start(out=out[b * P : (b + 1) * P, :], in_=res[:])
 
-        y_block(0, True)
-        y_block(1, True)
-        y_block(2, True)
+        prepare(0)
+        x_bytes = gather_scales("xb", xs)
+        x_picked = gather_words("xp", xw)
         e_bytes = gather_scales("eb", es)
-        e_planes = gather_words("ep", ew)
-        t0 = z_block(0, True)
-        t1 = z_block(1, True)
-        y_block(3, False)
-        finish(0, *t0)
-        t2 = z_block(2, True)
-        finish(1, *t1)
-        t3 = z_block(3, True)
-        finish(2, *t2)
-        finish(3, *t3)
+        e_picked = gather_words("ep", ew)
+        for b in range(1, NB):
+            prepare(b)
+        for b in range(NB):
+            multiply(b)
+        for b in range(NB):
+            combine(b)
+        for b in range(NB):
+            finish(b)

@@ -36,9 +36,9 @@ def tile_picked_yghost_norm_p_kernel(tc, x_words, x_scales, e_words, e_scales, h
             eng.memset(t[:].bitcast(I32), 0)
             return t
 
-        def load_scales(t, src, queue):
-            for q in range(4):
-                queue.dma_start(out=t[32 * q : 32 * q + 4, :].bitcast(I32), in_=src[0, 4 * q : 4 * q + 4, :].bitcast(I32))
+        def load_scales(t, src, queue, first_row):
+            for q in (0, 2, 1, 3):
+                queue.dma_start(out=t[32 * q + first_row : 32 * q + first_row + 4, :].bitcast(I32), in_=src[0, 4 * q : 4 * q + 4, :].bitcast(I32))
 
         def load_words(name, src):
             t = keep.tile([P, T], I32, name=name, align_bytes=64)
@@ -66,7 +66,7 @@ def tile_picked_yghost_norm_p_kernel(tc, x_words, x_scales, e_words, e_scales, h
 
         def cast(name, raw, eng):
             grouped = keep.tile([P, P, PACK], BF16, name=name, tag=name, align_bytes=64)
-            dst, src = grouped[:], raw[:].rearrange("p j w -> p w j")
+            dst, src = grouped[:].rearrange("p (c i) j -> p c j i", i=4), raw[:].rearrange("p j (c i) -> p c j i", i=4)
             if eng == "S":
                 nc.scalar.copy(out=dst, in_=src)
             elif eng == "G":
@@ -84,7 +84,7 @@ def tile_picked_yghost_norm_p_kernel(tc, x_words, x_scales, e_words, e_scales, h
         def product(tag, bufs, words, bytes_, q):
             acc = psum.tile([P, S], F32, name=tag, tag=tag, bufs=bufs)
             nc.tensor.matmul_mx(out=acc[:], lhsT=q[0][:].bitcast(FP8X4), lhsT_scale=q[1][:],
-                                rhs=words[:].bitcast(FP8X4), rhs_scale=bytes_[:], start=True, stop=True)
+                                rhs=words[:].bitcast(FP8X4), rhs_scale=bytes_, start=True, stop=True)
             return acc[:].rearrange("p (v d) -> p d v", d=D)
 
         xs = scale_table("xs", nc.vector)
@@ -95,20 +95,20 @@ def tile_picked_yghost_norm_p_kernel(tc, x_words, x_scales, e_words, e_scales, h
         g_raw = [None] * NB
         h_raw[0] = load_block("h0", hT, 0)
         g_raw[0] = load_block("g0", gT, 0)
-        load_scales(xs, x_scales, nc.sync)
+        load_scales(xs, x_scales, nc.sync, 0)
         xw = load_words("xw", x_words)
-        load_scales(es, e_scales, nc.sync)
+        load_scales(es, e_scales, nc.sync, 4)
         ew = load_words("ew", e_words)
-        load_steps(nc.sync)
         h_raw[1] = load_block("h1", hT, 1)
         g_raw[1] = load_block("g1", gT, 1)
         h_raw[2] = load_block("h2", hT, 2)
         g_raw[2] = load_block("g2", gT, 2)
         h_raw[3] = load_block("h3", hT, 3)
         g_raw[3] = load_block("g3", gT, 3)
+        load_steps(nc.sync)
 
         warm = keep.tile([P, 2], F32, name="warm")
-        nc.gpsimd.memset(warm[:, 0:1], 1.0)
+        nc.vector.memset(warm[:, 0:1], 1.0)
         nc.scalar.activation(out=warm[:, 1:2], in_=warm[:, 0:1], func=ACT.Abs_reciprocal_sqrt)
 
 
@@ -119,6 +119,8 @@ def tile_picked_yghost_norm_p_kernel(tc, x_words, x_scales, e_words, e_scales, h
         def tile(name, shape):
             return keep.tile(shape, F32, name=name, tag=SLOT.get(name, name), align_bytes=64)
 
+        step_sq = keep.tile([P, NB], F32, name="step_sq")
+        nc.gpsimd.tensor_tensor(out=step_sq[:], in0=step[:], in1=step[:], op=MULT)
         hq = [None] * NB
         gq = [None] * NB
         y_ps = [None] * NB
@@ -133,14 +135,14 @@ def tile_picked_yghost_norm_p_kernel(tc, x_words, x_scales, e_words, e_scales, h
             gq[b] = quantise("gq%d" % b, gc)
 
         def multiply(b):
-            y_ps[b] = product("y", 4, x_picked, x_bytes, hq[b])
-            z_ps[b] = product("z", 4, e_picked, e_bytes, gq[b])
+            y_ps[b] = product("y", 4, x_picked, x_bytes[:], hq[b])
+            z_ps[b] = product("z", 4, e_picked, e_bytes[4:P, :], gq[b])
 
         def combine(b):
             y_sb = tile("y%d" % b, [P, D, G])
             nc.scalar.copy(out=y_sb[:], in_=y_ps[b])
             terms[b] = tile("terms%d" % b, [P, D, G])
-            nc.vector.scalar_tensor_tensor(out=terms[b][:], in0=z_ps[b], scalar=step[:, b : b + 1], in1=y_sb[:], op0=MULT, op1=MULT)
+            nc.vector.tensor_tensor(out=terms[b][:], in0=z_ps[b], in1=y_sb[:], op=MULT)
             squares[b] = tile("squares%d" % b, [P, D, G])
             nc.scalar.activation(out=squares[b][:], in_=terms[b][:], func=ACT.Square)
 
@@ -154,9 +156,9 @@ def tile_picked_yghost_norm_p_kernel(tc, x_words, x_scales, e_words, e_scales, h
             sums = tile("sums%d" % b, [P, 2, G])
             nc.vector.tensor_tensor(out=sums[:], in0=halves[:, :, 0, :], in1=halves[:, :, 1, :], op=ADD)
             inv = tile("inv%d" % b, [P, G])
-            nc.scalar.activation(out=inv[:], in_=sums[:, 1, :], func=ACT.Abs_reciprocal_sqrt, bias=0.1)
+            nc.scalar.activation(out=inv[:], in_=sums[:, 1, :], func=ACT.Abs_reciprocal_sqrt, scale=step_sq[:, b : b + 1], bias=0.1)
             res = tile("res%d" % b, [P, G])
-            nc.vector.tensor_tensor(out=res[:], in0=sums[:, 0, :], in1=inv[:], op=MULT)
+            nc.vector.scalar_tensor_tensor(out=res[:], in0=sums[:, 0, :], scalar=step[:, b : b + 1], in1=inv[:], op0=MULT, op1=MULT)
             nc.sync.dma_start(out=out[b * P : (b + 1) * P, :], in_=res[:])
 
         prepare(0)

@@ -37,8 +37,8 @@ def tile_picked_yghost_norm_p_kernel(tc, x_words, x_scales, e_words, e_scales, h
             return t
 
         def load_scales(t, src, queue, first_row):
-            for q in (0, 2, 1, 3):
-                queue.dma_start(out=t[32 * q + first_row : 32 * q + first_row + 4, :].bitcast(I32), in_=src[0, 4 * q : 4 * q + 4, :].bitcast(I32))
+            for r in range(4):
+                queue.dma_start(out=t[first_row + r : P : 32, :].bitcast(I32), in_=src[0, r:16:4, :].bitcast(I32))
 
         def load_words(name, src):
             t = keep.tile([P, T], I32, name=name, align_bytes=64)
@@ -85,10 +85,10 @@ def tile_picked_yghost_norm_p_kernel(tc, x_words, x_scales, e_words, e_scales, h
             acc = psum.tile([P, S], F32, name=tag, tag=tag, bufs=bufs)
             nc.tensor.matmul_mx(out=acc[:], lhsT=q[0][:].bitcast(FP8X4), lhsT_scale=q[1][:],
                                 rhs=words[:].bitcast(FP8X4), rhs_scale=bytes_, start=True, stop=True)
-            return acc[:].rearrange("p (v d) -> p d v", d=D)
+            return acc[:]
 
-        xs = scale_table("xs", nc.vector)
-        es = scale_table("es", nc.gpsimd)
+        xs = scale_table("xs", nc.gpsimd)
+        es = scale_table("es", nc.vector)
         step = keep.tile([P, NB], F32, name="step")
 
         h_raw = [None] * NB
@@ -112,9 +112,9 @@ def tile_picked_yghost_norm_p_kernel(tc, x_words, x_scales, e_words, e_scales, h
         nc.scalar.activation(out=warm[:, 1:2], in_=warm[:, 0:1], func=ACT.Abs_reciprocal_sqrt)
 
 
-        CAST = "SSSSSVVV"
+        CAST = "SSSSSVSV"
         ROUTE = "VVVV"
-        SLOT = {"y1":"h2","y2":"h3","squares0":"hc3","terms0":"gc1","terms1":"gc2","halves0":"gc3"}
+        SLOT = {"y1":"h2","y2":"h3","squares0":"hc2","squares1":"hc3","terms0":"gc1","terms1":"gc2","terms2":"gc3"}
 
         def tile(name, shape):
             return keep.tile(shape, F32, name=name, tag=SLOT.get(name, name), align_bytes=64)
@@ -139,22 +139,23 @@ def tile_picked_yghost_norm_p_kernel(tc, x_words, x_scales, e_words, e_scales, h
             z_ps[b] = product("z", 4, e_picked, e_bytes[4:P, :], gq[b])
 
         def combine(b):
-            y_sb = tile("y%d" % b, [P, D, G])
+            y_sb = tile("y%d" % b, [P, S])
             nc.scalar.copy(out=y_sb[:], in_=y_ps[b])
-            terms[b] = tile("terms%d" % b, [P, D, G])
+            terms[b] = tile("terms%d" % b, [P, S])
             nc.vector.tensor_tensor(out=terms[b][:], in0=z_ps[b], in1=y_sb[:], op=MULT)
-            squares[b] = tile("squares%d" % b, [P, D, G])
+            squares[b] = tile("squares%d" % b, [P, S])
             nc.scalar.activation(out=squares[b][:], in_=terms[b][:], func=ACT.Square)
 
         def finish(b):
             finish_on_vector(b)
 
         def finish_on_vector(b):
-            halves = tile("halves%d" % b, [P, 2, 2, G])
+            halves = tile("halves%d" % b, [P, 2, G, 2])
             for i, src in enumerate((terms[b], squares[b])):
-                nc.vector.tensor_tensor(out=halves[:, i], in0=src[:, 0:2, :], in1=src[:, 2:4, :], op=ADD) if i == 0 else nc.vector.tensor_tensor(out=halves[:, i], in0=src[:, 0:2, :], in1=src[:, 2:4, :], op=ADD)
+                quads = src[:].rearrange("p (v d) -> p v d", d=D)
+                nc.vector.tensor_tensor(out=halves[:, i], in0=quads[:, :, 0:2], in1=quads[:, :, 2:4], op=ADD)
             sums = tile("sums%d" % b, [P, 2, G])
-            nc.vector.tensor_tensor(out=sums[:], in0=halves[:, :, 0, :], in1=halves[:, :, 1, :], op=ADD)
+            nc.vector.tensor_tensor(out=sums[:], in0=halves[:, :, :, 0], in1=halves[:, :, :, 1], op=ADD)
             inv = tile("inv%d" % b, [P, G])
             nc.scalar.activation(out=inv[:], in_=sums[:, 1, :], func=ACT.Abs_reciprocal_sqrt, scale=step_sq[:, b : b + 1], bias=0.1)
             res = tile("res%d" % b, [P, G])

from contextlib import ExitStack

import concourse.mybir as mybir

K, T, S, V, D = 512, 2048, 512, 512, 4
FLOPS = 2 * 2 * K * V * S

F32 = mybir.dt.float32
BF16 = mybir.dt.bfloat16
I32 = mybir.dt.int32
U32 = mybir.dt.uint32
U16 = mybir.dt.uint16
U8 = mybir.dt.uint8
FP8X4 = mybir.dt.float8_e4m3fn_x4
ACT = mybir.ActivationFunctionType
MULT = mybir.AluOpType.mult
ADD = mybir.AluOpType.add

P = 128
PACK = 4
NB = V // P
G = S // D


def tile_picked_yghost_norm_p_kernel(tc, x_words, x_scales, e_words, e_scales, hT, gT, lr, offs, out):
    nc = tc.nc
    with ExitStack() as ctx:
        keep = ctx.enter_context(tc.tile_pool(name="keep", bufs=1))
        psum = ctx.enter_context(tc.psum_pool(name="psum", bufs=1))

        offsets = keep.tile([P, S // 16], U16, name="offsets")
        nc.sync.dma_start(offsets[:], offs)

        def scale_table(name, eng):
            t = keep.tile([P, T], U8, name=name, align_bytes=64)
            eng.memset(t[:].bitcast(I32), 0)
            return t

        def load_scales(t, src, queue, first_row):
            for r in range(4):
                queue.dma_start(out=t[first_row + r : P : 32, :].bitcast(I32), in_=src[0, r:16:4, :].bitcast(I32))

        def load_words(name, src):
            t = keep.tile([P, T], I32, name=name, align_bytes=64)
            nc.sync.dma_start(out=t[:], in_=src[0].rearrange("p n t -> p (n t)").bitcast(I32))
            return t

        def load_block(name, src, b):
            t = keep.tile([P, PACK, P], F32, name=name, tag=name, align_bytes=64)
            nc.sync.dma_start(out=t[:], in_=src[:, b * P : (b + 1) * P].rearrange("(p j) w -> p j w", j=PACK))
            return t

        def load_steps(queue):
            with nc.allow_non_contiguous_dma(reason="one step size a partition"):
                queue.dma_start(out=step[:], in_=lr.rearrange("(b p) o -> p (b o)", p=P))

        def gather_scales(name, table):
            picked = keep.tile([P, S], U8, name=name, align_bytes=64)
            nc.vector.tensor_copy(out=picked[:], in_=table[:].indirect(offsets[:]))
            return picked

        def gather_words(name, table):
            picked = keep.tile([P, S], U32, name=name, align_bytes=64)
            nc.vector.tensor_copy(out=picked[:], in_=table[:].bitcast(U32).indirect(offsets[:]))
            return picked

        def cast(name, raw, eng):
            grouped = keep.tile([P, P, PACK], BF16, name=name, tag=name, align_bytes=64)
            dst, src = grouped[:].rearrange("p (c i) j -> p c j i", i=4), raw[:].rearrange("p j (c i) -> p c j i", i=4)
            if eng == "S":
                nc.scalar.copy(out=dst, in_=src)
            elif eng == "G":
                nc.gpsimd.tensor_copy(out=dst, in_=src)
            else:
                nc.vector.tensor_copy(out=dst, in_=src)
            return grouped

        def quantise(name, grouped):
            codes = keep.tile([P, P], U32, name=name + "_codes", align_bytes=64)
            scales = keep.tile([P, P], U8, name=name + "_scales", align_bytes=64)
            nc.vector.quantize_mx(out=codes[:].bitcast(FP8X4), scales=scales[:], in_=grouped[:].rearrange("p w j -> p (w j)"))
            return codes, scales

        def product(tag, bufs, words, bytes_, q):
            acc = psum.tile([P, S], F32, name=tag, tag=tag, bufs=bufs)
            nc.tensor.matmul_mx(out=acc[:], lhsT=q[0][:].bitcast(FP8X4), lhsT_scale=q[1][:],
                                rhs=words[:].bitcast(FP8X4), rhs_scale=bytes_, start=True, stop=True)
            return acc[:]

        xs = scale_table("xs", nc.gpsimd)
        es = scale_table("es", nc.vector)
        step = keep.tile([P, NB], F32, name="step")

        h_raw = [None] * NB
        g_raw = [None] * NB
        h_raw[0] = load_block("h0", hT, 0)
        g_raw[0] = load_block("g0", gT, 0)
        load_scales(xs, x_scales, nc.sync, 0)
        xw = load_words("xw", x_words)
        load_scales(es, e_scales, nc.sync, 4)
        ew = load_words("ew", e_words)
        h_raw[1] = load_block("h1", hT, 1)
        g_raw[1] = load_block("g1", gT, 1)
        h_raw[2] = load_block("h2", hT, 2)
        g_raw[2] = load_block("g2", gT, 2)
        h_raw[3] = load_block("h3", hT, 3)
        g_raw[3] = load_block("g3", gT, 3)
        load_steps(nc.sync)

        warm = keep.tile([P, 2], F32, name="warm")
        nc.vector.memset(warm[:, 0:1], 1.0)
        nc.scalar.activation(out=warm[:, 1:2], in_=warm[:, 0:1], func=ACT.Abs_reciprocal_sqrt)


        CAST = "SSSSSVSV"
        ROUTE = "VVVV"
        SLOT = {"y1":"h2","y2":"h3","squares0":"hc2","squares1":"hc3","terms0":"gc1","terms1":"gc2","terms2":"gc3"}

        def tile(name, shape):
            return keep.tile(shape, F32, name=name, tag=SLOT.get(name, name), align_bytes=64)

        step_sq = keep.tile([P, NB], F32, name="step_sq")
        nc.gpsimd.tensor_tensor(out=step_sq[:], in0=step[:], in1=step[:], op=MULT)
        hq = [None] * NB
        gq = [None] * NB
        y_ps = [None] * NB
        z_ps = [None] * NB
        terms = [None] * NB
        squares = [None] * NB

        def prepare(b):
            hc = cast("hc%d" % b, h_raw[b], CAST[b])
            gc = cast("gc%d" % b, g_raw[b], CAST[NB + b])
            hq[b] = quantise("hq%d" % b, hc)
            gq[b] = quantise("gq%d" % b, gc)

        def multiply(b):
            y_ps[b] = product("y", 4, x_picked, x_bytes[:], hq[b])
            z_ps[b] = product("z", 4, e_picked, e_bytes[4:P, :], gq[b])

        def combine(b):
            y_sb = tile("y%d" % b, [P, S])
            nc.scalar.copy(out=y_sb[:], in_=y_ps[b])
            terms[b] = tile("terms%d" % b, [P, S])
            nc.vector.tensor_tensor(out=terms[b][:], in0=z_ps[b], in1=y_sb[:], op=MULT)
            squares[b] = tile("squares%d" % b, [P, S])
            nc.scalar.activation(out=squares[b][:], in_=terms[b][:], func=ACT.Square)

        def finish(b):
            finish_on_vector(b)

        def finish_on_vector(b):
            halves = tile("halves%d" % b, [P, 2, G, 2])
            for i, src in enumerate((terms[b], squares[b])):
                quads = src[:].rearrange("p (v d) -> p v d", d=D)
                nc.vector.tensor_tensor(out=halves[:, i], in0=quads[:, :, 0:2], in1=quads[:, :, 2:4], op=ADD)
            sums = tile("sums%d" % b, [P, 2, G])
            nc.vector.tensor_tensor(out=sums[:], in0=halves[:, :, :, 0], in1=halves[:, :, :, 1], op=ADD)
            inv = tile("inv%d" % b, [P, G])
            nc.scalar.activation(out=inv[:], in_=sums[:, 1, :], func=ACT.Abs_reciprocal_sqrt, scale=step_sq[:, b : b + 1], bias=0.1)
            res = tile("res%d" % b, [P, G])
            nc.vector.scalar_tensor_tensor(out=res[:], in0=sums[:, 0, :], scalar=step[:, b : b + 1], in1=inv[:], op0=MULT, op1=MULT)
            nc.sync.dma_start(out=out[b * P : (b + 1) * P, :], in_=res[:])

        prepare(0)
        x_bytes = gather_scales("xb", xs)
        x_picked = gather_words("xp", xw)
        e_bytes = gather_scales("eb", es)
        e_picked = gather_words("ep", ew)
        for b in range(1, NB):
            prepare(b)
        for b in range(NB):
            multiply(b)
        for b in range(NB):
            combine(b)
        for b in range(NB):
            finish(b)
